import numpy as np
import ml_dtypes


def mxq(x, axis, fmt="e4m3"):
    dtype, down = {"e4m3": (ml_dtypes.float8_e4m3fn, 7), "e5m2": (ml_dtypes.float8_e5m2, 14)}[fmt]
    v = np.moveaxis(np.asarray(x, np.float32).astype(ml_dtypes.bfloat16).astype(np.float64), axis, -1)
    blocks = v.reshape(v.shape[:-1] + (-1, 32))
    amax = np.abs(blocks).max(-1, keepdims=True)
    byte = np.maximum(np.where(amax > 0, np.frexp(amax)[1] - 1 + 127, 0) - down, 1)
    scale = np.exp2(byte - 127.0)
    codes = (blocks / scale).astype(np.float32).astype(dtype).astype(np.float64)
    return np.moveaxis((codes * scale).reshape(v.shape), -1, axis)


WIDE = False


def mx_kscale(k):
    if not WIDE:
        return np.ones(k)
    levels = np.array([10, -10, 5, -5, 0])
    if k % 512:
        return np.exp2(np.random.permutation(np.resize(levels, k // 32))).repeat(32)
    a = np.empty((k // 512, 16))
    for p in range(k // 512):
        a[p, :8] = np.random.permutation(np.resize(levels, 8))
        for g in range(8):
            far = levels[np.abs(levels - a[p, g]) >= 10]
            a[p, g + 8] = far[np.random.randint(len(far))]
    return np.exp2(a.ravel()).repeat(32)


def f64(x):
    return np.asarray(x).astype(np.float64)


def striped(idx):
    return np.tile(idx.reshape(-1, 16).T, (8, 1)).astype(np.uint16)


def unstriped(offs):
    return offs[:16].T.reshape(-1).astype(np.int64)


def pack_weight(w):
    k, n = w.shape
    w = f64(np.asarray(w, np.float32).astype(ml_dtypes.bfloat16)).reshape(k // 32, 32, n)
    amax = np.abs(w).max(1)
    byte = np.clip(np.where(amax > 0, np.frexp(amax)[1] - 1 + 127 - 7, 1), 1, 254)
    scaled = (w * np.exp2(127.0 - byte)[:, None, :]).reshape(k, n).astype(np.float32)
    words = np.ascontiguousarray(scaled.reshape(k // 512, 128, 4, n).transpose(0, 1, 3, 2)).astype(ml_dtypes.float8_e4m3fn).view(np.uint8)
    return words, np.ascontiguousarray(byte.astype(np.uint8).reshape(k // 512, 16, n))


def unpack_weight(words, scales):
    g, p, n, _ = words.shape
    vals = np.ascontiguousarray(words).view(ml_dtypes.float8_e4m3fn).astype(np.float64) * np.repeat(np.exp2(scales.astype(np.float64) - 127.0), 8, axis=1)[..., None]
    return vals.transpose(0, 1, 3, 2).reshape(g * 512, n)


K, T, S, N, R = 512, 2048, 512, 256, 256


def setup_inputs():
    n = np.random.standard_normal
    s = mx_kscale(K)[:, None]
    c = mx_kscale(S)
    packed_xT = pack_weight(n((K, T)) * s)
    packed_eT = pack_weight(n((K, T)) * s)
    return {
        "x_words": packed_xT[0],
        "x_scales": packed_xT[1],
        "e_words": packed_eT[0],
        "e_scales": packed_eT[1],
        "xr": (n((K, N)) / np.sqrt(K) / s).astype(np.float32),
        "xi": (n((K, N)) / np.sqrt(K) / s).astype(np.float32),
        "amp": (np.random.uniform(0.3, 2.0, (S, N))).astype(np.float32),
        "wgt": (np.random.uniform(0.5, 1.0, (S, 1)) * c[:, None]).astype(np.float32),
        "br": (n((S, R)) / np.sqrt(2 * S) / c[:, None]).astype(np.float32),
        "bi": (n((S, R)) / np.sqrt(2 * S) / c[:, None]).astype(np.float32),
        "cur": (n((R, N))).astype(np.float32),
        "offs": striped(np.random.permutation(T)[:S]),
    }


def reference(x_words, x_scales, e_words, e_scales, xr, xi, amp, wgt, br, bi, cur, offs):
    xq = unpack_weight(x_words, x_scales)[:, unstriped(offs)]
    xrq = mxq(f64(xr), 0, "e4m3")
    e_offs = unpack_weight(e_words, e_scales)[:, unstriped(offs)]
    xiq = mxq(f64(xi), 0, "e4m3")
    z = e_offs.T @ xiq
    re = (xq.T @ xrq) - z
    im = xq.T @ xiq + e_offs.T @ xrq
    cf = f64(wgt) * (-1.0 * (f64(amp) / (np.sqrt((re) ** 2 + (im) ** 2 + 0.1))) + 1.0)
    zr = cf * re
    zi = cf * im
    return f64(cur) - (0.5 * ((mxq(f64(br), 0, "e4m3").T @ mxq(zr, 0, "e4m3") + mxq(f64(bi), 0, "e4m3").T @ mxq(zi, 0, "e4m3"))))

@@ -1,0 +1,261 @@
+from contextlib import ExitStack
+
+import concourse.mybir as mybir
+
+K, T, S, N, R = 512, 2048, 512, 256, 256
+FLOPS = 2 * (4 * K * S * N + 2 * S * R * N)
+
+F32 = mybir.dt.float32
+BF16 = mybir.dt.bfloat16
+I32 = mybir.dt.int32
+U32 = mybir.dt.uint32
+U16 = mybir.dt.uint16
+U8 = mybir.dt.uint8
+FP8X4 = mybir.dt.float8_e4m3fn_x4
+ACT = mybir.ActivationFunctionType
+ALU = mybir.AluOpType
+
+P = 128
+PACK = 4
+HALF = 128
+QUART = 64
+
+
+def tile_picked_yaflow_step_p_kernel(
+    tc, x_words, x_scales, e_words, e_scales, xr, xi, amp, wgt, br, bi, cur, offs, out
+):
+    nc = tc.nc
+    with ExitStack() as ctx:
+        sb = ctx.enter_context(tc.tile_pool(name="sb", bufs=1))
+        ps = ctx.enter_context(tc.psum_pool(name="ps", bufs=1))
+
+        def tile(shape, dtype, name):
+            return sb.tile(shape, dtype, name=name, align_bytes=64)
+
+        def cleared(name, clear):
+            table = tile([P, T], U8, name)
+            clear.memset(table[:].bitcast(I32), 0)
+            return table
+
+        offsets = sb.tile([P, S // 16], U16, name="offsets")
+        nc.sync.dma_start(offsets[:], offs)
+
+        xs_table = cleared("xs_table", nc.vector)
+        es_table = cleared("es_table", nc.gpsimd)
+        one = tile([P, 1], F32, "one")
+        warm = tile([P, 1], F32, "warm")
+        nc.vector.memset(one[:], 1.0)
+        nc.scalar.activation(warm[:], one[:], ACT.Abs_reciprocal_sqrt)
+
+        def load_scales(table, scales):
+            for q in range(4):
+                nc.sync.dma_start(table[32 * q : 32 * q + 4, :].bitcast(I32), scales[0, 4 * q : 4 * q + 4, :].bitcast(I32))
+
+        def load_words(name, words):
+            table = tile([P, T], I32, name)
+            nc.sync.dma_start(table[:], words[0].rearrange("p c b -> p (c b)").bitcast(I32))
+            return table
+
+        def load_rows(name, rows):
+            raw = tile([P, PACK, rows.shape[1]], F32, name)
+            nc.sync.dma_start(raw[:], rows.rearrange("(p j) c -> p j c", j=PACK))
+            return raw
+
+        xr_raw = load_rows("xr_raw", xr)
+        load_scales(xs_table, x_scales)
+        xw_table = load_words("xw_table", x_words)
+        load_scales(es_table, e_scales)
+        xi_raw = load_rows("xi_raw", xi)
+        ew_table = load_words("ew_table", e_words)
+        w_sb = tile([P, PACK], F32, "w_sb")
+        nc.gpsimd.dma_start(w_sb[:], wgt.rearrange("(p j) o -> p (j o)", j=PACK))
+        br_raw = load_rows("br_raw", br)
+        bi_raw = load_rows("bi_raw", bi)
+        amp_sb = load_rows("amp_sb", amp)
+        cur_sb = tile([P, R // P, N], F32, "cur_sb")
+        nc.sync.dma_start(cur_sb[:], cur.rearrange("(t p) m -> p t m", p=P))
+        neg_w = tile([P, PACK], F32, "neg_w")
+        nc.gpsimd.tensor_scalar(neg_w[:], w_sb[:], -1.0, 0.0, ALU.mult, ALU.add)
+
+        def gather_scales(name, table):
+            picked = tile([P, S], U8, name)
+            nc.vector.tensor_copy(picked[:], table[:].indirect(offsets[:]))
+            return picked
+
+        def deal_scales(name, picked):
+            dealt = tile([P, S], U8, name)
+            nc.vector.tensor_copy(dealt[:].rearrange("p (j q) -> p j q", j=PACK), picked[:].rearrange("p (q j) -> p j q", j=PACK))
+            return dealt
+
+        def gather_words(name, table):
+            dealt = tile([P, S], U32, name)
+            nc.vector.tensor_copy(dealt[:].rearrange("p (j q) -> p q j", j=PACK), table[:].bitcast(U32).indirect(offsets[:]))
+            return dealt
+
+        def woven(ap):
+            return ap.rearrange("p (c i j) -> p c j i", i=4, j=PACK)
+
+        def planar(ap):
+            return ap.rearrange("p j (c i) -> p c j i", i=4)
+
+        def cast(name, raw_cols, scale):
+            width = raw_cols.shape[2]
+            grouped = tile([P, width * PACK], BF16, name)
+            nc.scalar.activation(woven(grouped[:]), planar(raw_cols), ACT.Copy, scale=scale)
+            return grouped
+
+        def quantize(name, grouped):
+            width = grouped.shape[1] // PACK
+            codes = tile([P, width], U32, name + "_codes")
+            scales = tile([P, width], U8, name + "_scales")
+            nc.vector.quantize_mx(out=codes[:].bitcast(FP8X4), scales=scales[:], in_=grouped[:])
+            return codes, scales
+
+        def mm(acc, lhs, lhs_cols, rhs, rhs_cols, start, stop):
+            nc.tensor.matmul_mx(
+                out=acc,
+                lhsT=lhs[0][:, lhs_cols].bitcast(FP8X4),
+                lhsT_scale=lhs[1][:, lhs_cols],
+                rhs=rhs[0][:, rhs_cols].bitcast(FP8X4),
+                rhs_scale=rhs[1][:, rhs_cols],
+                start=start,
+                stop=stop,
+            )
+
+        halves = [slice(h * HALF, (h + 1) * HALF) for h in range(N // HALF)]
+        quarters = [slice(q * QUART, (q + 1) * QUART) for q in range(N // QUART)]
+        NEG_XI, XR, XI = 0, 1, 2
+        sig_bf = [tile([P, 2 * 3 * QUART * PACK], BF16, "sig_bf%d" % h) for h in range(2)]
+        sig_codes = [tile([P, 2 * 3 * QUART], U32, "sig_codes%d" % h) for h in range(2)]
+        sig_scales = [tile([P, 2 * 3 * QUART], U8, "sig_scales%d" % h) for h in range(2)]
+
+        def sig_slot(h, slot):
+            return sig_bf[h][:].rearrange("p (q s c i j) -> p q s c j i", q=2, s=3, i=4, j=PACK)[:, :, slot]
+
+        def sig_src(raw, h):
+            return raw[:, :, halves[h]].rearrange("p j (q c i) -> p q c j i", q=2, i=4)
+
+        def cast_xi(h):
+            nc.scalar.copy(sig_slot(h, XI), sig_src(xi_raw, h))
+            for q in range(2):
+                nc.scalar.activation(sig_slot(h, NEG_XI)[:, q], sig_src(xi_raw, h)[:, q], ACT.Copy, scale=-1.0)
+
+        def quantize_sig(h, lo, hi):
+            nc.vector.quantize_mx(
+                out=sig_codes[h][:, lo:hi].bitcast(FP8X4), scales=sig_scales[h][:, lo:hi], in_=sig_bf[h][:, lo * PACK : hi * PACK]
+            )
+
+        xs_picked = gather_scales("xs_picked", xs_table)
+        for h in range(2):
+            nc.scalar.copy(sig_slot(h, XR), sig_src(xr_raw, h))
+        xs = deal_scales("xs", xs_picked)
+        xw = gather_words("xw", xw_table)
+        es_picked = gather_scales("es_picked", es_table)
+        cast_xi(0)
+        quantize_sig(0, 0, 256)
+        es = deal_scales("es", es_picked)
+        quantize_sig(0, 256, 384)
+        ew = gather_words("ew", ew_table)
+        cast_xi(1)
+        quantize_sig(1, 0, 256)
+        quantize_sig(1, 256, 384)
+        x_q = (xw, xs)
+        e_q = (ew, es)
+
+        field = []
+        for q in range(4):
+            sig_q = (sig_codes[q // 2], sig_scales[q // 2])
+            base = (q % 2) * 3 * QUART
+            bank = ps.tile([P, PACK, 2 * QUART], F32, name="field%d" % q)
+            for j in range(PACK):
+                rows = slice(j * P, (j + 1) * P)
+                mm(bank[:, j, :], x_q, rows, sig_q, slice(base + QUART, base + 3 * QUART), True, False)
+                mm(bank[:, j, :], e_q, rows, sig_q, slice(base, base + 2 * QUART), False, True)
+            field.append(bank)
+
+        br_q = quantize("br_q", cast("br_bf", br_raw[:], 1.0))
+        bi_bf = tile([P, R * PACK], BF16, "bi_bf")
+        nc.vector.tensor_copy(woven(bi_bf[:]), planar(bi_raw[:]))
+
+        squares = [tile([P, PACK, 2 * QUART], F32, "squares%d" % q) for q in range(4)]
+        power = [tile([P, PACK, QUART], F32, "power%d" % q) for q in range(4)]
+        inv = [tile([P, PACK, QUART], F32, "inv%d" % q) for q in range(4)]
+        ratio = [tile([P, PACK, QUART], F32, "ratio%d" % q) for q in range(4)]
+        coef = [tile([P, PACK, QUART], F32, "coef%d" % q) for q in range(4)]
+        z_bf = [tile([P, 2 * HALF * PACK], BF16, "z_bf%d" % h) for h in range(2)]
+        b_q = [br_q]
+        z_q = []
+
+        def square(q):
+            nc.scalar.activation(squares[q][:], field[q][:], ACT.Square)
+
+        def add_squares(q):
+            nc.vector.scalar_tensor_tensor(power[q][:], squares[q][:, :, :QUART], 0.1, squares[q][:, :, QUART:], ALU.add, ALU.add)
+
+        def inverse_root(q):
+            nc.scalar.activation(inv[q][:], power[q][:], ACT.Abs_reciprocal_sqrt)
+
+        def amp_ratio(q):
+            nc.vector.tensor_tensor(ratio[q][:], inv[q][:], amp_sb[:, :, quarters[q]], ALU.mult)
+
+        def coefficient(q):
+            for j in range(PACK):
+                nc.scalar.activation(coef[q][:, j, :], ratio[q][:, j, :], ACT.Identity, bias=w_sb[:, j : j + 1], scale=neg_w[:, j : j + 1])
+
+        def residual(q):
+            for s in range(2):
+                lo = (s * HALF + (q % 2) * QUART) * PACK
+                nc.vector.tensor_tensor(
+                    woven(z_bf[q // 2][:, lo : lo + QUART * PACK]),
+                    planar(field[q][:, :, s * QUART : (s + 1) * QUART]),
+                    planar(coef[q][:]),
+                    ALU.mult,
+                )
+
+        def back(h):
+            z_h = quantize("z_q%d" % h, z_bf[h])
+            accs = []
+            for t in range(R // P):
+                rows = slice(t * P, (t + 1) * P)
+                acc = ps.tile([P, HALF], F32, name="acc%d_%d" % (h, t))
+                mm(acc[:], b_q[0], rows, z_h, slice(0, HALF), True, False)
+                mm(acc[:], b_q[1], rows, z_h, slice(HALF, 2 * HALF), False, True)
+                accs.append(acc)
+            z_q.append(accs)
+
+        def finish(h):
+            for t in range(R // P):
+                res = tile([P, HALF], F32, "res%d_%d" % (h, t))
+                nc.vector.scalar_tensor_tensor(res[:], z_q[h][t][:], -0.5, cur_sb[:, t, halves[h]], ALU.mult, ALU.add)
+                queue = nc.sync if t == 0 else nc.scalar
+                queue.dma_start(out[t * P : (t + 1) * P, halves[h]], res[:])
+
+        square(0)
+        add_squares(0)
+        b_q.append(quantize("bi_q", bi_bf))
+        square(1)
+        inverse_root(0)
+        add_squares(1)
+        amp_ratio(0)
+        square(2)
+        inverse_root(1)
+        coefficient(0)
+        add_squares(2)
+        amp_ratio(1)
+        residual(0)
+        square(3)
+        inverse_root(2)
+        coefficient(1)
+        add_squares(3)
+        amp_ratio(2)
+        residual(1)
+        inverse_root(3)
+        coefficient(2)
+        amp_ratio(3)
+        back(0)
+        coefficient(3)
+        residual(2)
+        residual(3)
+        finish(0)
+        back(1)
+        finish(1)

@@ -29,63 +29,59 @@ def tile_picked_yaflow_step_p_kernel(
         sb = ctx.enter_context(tc.tile_pool(name="sb", bufs=1))
         ps = ctx.enter_context(tc.psum_pool(name="ps", bufs=1))
 
-        def tile(shape, dtype, name):
-            return sb.tile(shape, dtype, name=name, align_bytes=64)
+        def tile(shape, dtype, name, tag=None):
+            return sb.tile(shape, dtype, name=name, tag=tag or name, align_bytes=64)
 
-        def cleared(name, clear):
-            table = tile([P, T], U8, name)
+        def cleared(name, width, clear):
+            table = tile([P, width], U8, name)
             clear.memset(table[:].bitcast(I32), 0)
             return table
 
         offsets = sb.tile([P, S // 16], U16, name="offsets")
         nc.sync.dma_start(offsets[:], offs)
 
-        xs_table = cleared("xs_table", nc.vector)
-        es_table = cleared("es_table", nc.gpsimd)
+        xs_table = cleared("xs_table", T, nc.vector)
+        es_table = cleared("es_table", T, nc.gpsimd)
+        planes = cleared("planes", 2 * S, nc.gpsimd)
         one = tile([P, 1], F32, "one")
         warm = tile([P, 1], F32, "warm")
         nc.vector.memset(one[:], 1.0)
         nc.scalar.activation(warm[:], one[:], ACT.Abs_reciprocal_sqrt)
 
         def load_scales(table, scales):
-            for q in range(4):
-                nc.sync.dma_start(table[32 * q : 32 * q + 4, :].bitcast(I32), scales[0, 4 * q : 4 * q + 4, :].bitcast(I32))
+            nc.sync.dma_start(table[0:P:8, :].bitcast(I32), scales[0].bitcast(I32))
 
         def load_words(name, words):
             table = tile([P, T], I32, name)
             nc.sync.dma_start(table[:], words[0].rearrange("p c b -> p (c b)").bitcast(I32))
             return table
 
-        def load_rows(name, rows):
-            raw = tile([P, PACK, rows.shape[1]], F32, name)
+        def load_rows(name, rows, tag=None):
+            raw = tile([P, PACK, rows.shape[1]], F32, name, tag)
             nc.sync.dma_start(raw[:], rows.rearrange("(p j) c -> p j c", j=PACK))
             return raw
 
-        xr_raw = load_rows("xr_raw", xr)
+        w_sb = tile([P, PACK, 1], F32, "w_sb")
+        nc.sync.dma_start(w_sb[:], wgt.rearrange("(p j) o -> p j o", j=PACK))
         load_scales(xs_table, x_scales)
-        xw_table = load_words("xw_table", x_words)
         load_scales(es_table, e_scales)
+        xr_raw = load_rows("xr_raw", xr)
+        xw_table = load_words("xw_table", x_words)
         xi_raw = load_rows("xi_raw", xi)
         ew_table = load_words("ew_table", e_words)
-        w_sb = tile([P, PACK], F32, "w_sb")
-        nc.gpsimd.dma_start(w_sb[:], wgt.rearrange("(p j) o -> p (j o)", j=PACK))
         br_raw = load_rows("br_raw", br)
         bi_raw = load_rows("bi_raw", bi)
-        amp_sb = load_rows("amp_sb", amp)
-        cur_sb = tile([P, R // P, N], F32, "cur_sb")
-        nc.sync.dma_start(cur_sb[:], cur.rearrange("(t p) m -> p t m", p=P))
-        neg_w = tile([P, PACK], F32, "neg_w")
+        neg_w = tile([P, PACK, 1], F32, "neg_w")
         nc.gpsimd.tensor_scalar(neg_w[:], w_sb[:], -1.0, 0.0, ALU.mult, ALU.add)
+        dealt = tile([P, 2 * S], U8, "dealt")
 
         def gather_scales(name, table):
             picked = tile([P, S], U8, name)
             nc.vector.tensor_copy(picked[:], table[:].indirect(offsets[:]))
             return picked
 
-        def deal_scales(name, picked):
-            dealt = tile([P, S], U8, name)
-            nc.vector.tensor_copy(dealt[:].rearrange("p (j q) -> p j q", j=PACK), picked[:].rearrange("p (q j) -> p j q", j=PACK))
-            return dealt
+        def deal_scales(cols, picked):
+            nc.vector.tensor_copy(dealt[:, cols].rearrange("p (j q) -> p j q", j=PACK), picked[:].rearrange("p (q j) -> p j q", j=PACK))
 
         def gather_words(name, table):
             dealt = tile([P, S], U32, name)
@@ -146,21 +142,26 @@ def tile_picked_yaflow_step_p_kernel(
             )
 
         xs_picked = gather_scales("xs_picked", xs_table)
+        es_picked = gather_scales("es_picked", es_table)
+        deal_scales(slice(0, S), xs_picked)
+        deal_scales(slice(S, 2 * S), es_picked)
         for h in range(2):
             nc.scalar.copy(sig_slot(h, XR), sig_src(xr_raw, h))
-        xs = deal_scales("xs", xs_picked)
+        for i in range(4):
+            nc.scalar.dma_start(planes[i:P:32, :].bitcast(I32), dealt[8 * i : P : 32, :].bitcast(I32))
+        cur_sb = tile([P, R // P, N], F32, "cur_sb", "xr_raw")
+        nc.sync.dma_start(cur_sb[:], cur.rearrange("(t p) m -> p t m", p=P))
         xw = gather_words("xw", xw_table)
-        es_picked = gather_scales("es_picked", es_table)
         cast_xi(0)
         quantize_sig(0, 0, 256)
-        es = deal_scales("es", es_picked)
         quantize_sig(0, 256, 384)
         ew = gather_words("ew", ew_table)
         cast_xi(1)
+        amp_sb = load_rows("amp_sb", amp, "xi_raw")
         quantize_sig(1, 0, 256)
         quantize_sig(1, 256, 384)
-        x_q = (xw, xs)
-        e_q = (ew, es)
+        x_q = (xw, planes[:, :S])
+        e_q = (ew, planes[:, S:])
 
         field = []
         for q in range(4):
@@ -199,8 +200,11 @@ def tile_picked_yaflow_step_p_kernel(
             nc.vector.tensor_tensor(ratio[q][:], inv[q][:], amp_sb[:, :, quarters[q]], ALU.mult)
 
         def coefficient(q):
+            if q < 2:
+                nc.vector.scalar_tensor_tensor(coef[q][:], ratio[q][:], 1.0, neg_w[:].to_broadcast([P, PACK, QUART]), ALU.subtract, ALU.mult)
+                return
             for j in range(PACK):
-                nc.scalar.activation(coef[q][:, j, :], ratio[q][:, j, :], ACT.Identity, bias=w_sb[:, j : j + 1], scale=neg_w[:, j : j + 1])
+                nc.scalar.activation(coef[q][:, j, :], ratio[q][:, j, :], ACT.Identity, bias=w_sb[:, j, :], scale=neg_w[:, j, :])
 
         def residual(q):
             for s in range(2):
@@ -239,22 +243,22 @@ def tile_picked_yaflow_step_p_kernel(
         amp_ratio(0)
         square(2)
         inverse_root(1)
-        coefficient(0)
         add_squares(2)
+        coefficient(0)
         amp_ratio(1)
-        residual(0)
         square(3)
         inverse_root(2)
-        coefficient(1)
         add_squares(3)
+        coefficient(1)
         amp_ratio(2)
-        residual(1)
         inverse_root(3)
+        residual(0)
         coefficient(2)
         amp_ratio(3)
-        back(0)
+        residual(1)
         coefficient(3)
         residual(2)
+        back(0)
         residual(3)
         finish(0)
         back(1)

@@ -42,7 +42,6 @@ def tile_picked_yaflow_step_p_kernel(
 
         xs_table = cleared("xs_table", T, nc.vector)
         es_table = cleared("es_table", T, nc.gpsimd)
-        planes = cleared("planes", 2 * S, nc.gpsimd)
         one = tile([P, 1], F32, "one")
         warm = tile([P, 1], F32, "warm")
         nc.vector.memset(one[:], 1.0)
@@ -84,15 +83,22 @@ def tile_picked_yaflow_step_p_kernel(
             nc.vector.tensor_copy(dealt[:, cols].rearrange("p (j q) -> p j q", j=PACK), picked[:].rearrange("p (q j) -> p j q", j=PACK))
 
         def gather_words(name, table):
-            dealt = tile([P, S], U32, name)
-            nc.vector.tensor_copy(dealt[:].rearrange("p (j q) -> p q j", j=PACK), table[:].bitcast(U32).indirect(offsets[:]))
-            return dealt
+            picked = [tile([P, S // 2], U32, name + "_picked%d" % u) for u in range(2)]
+            words = tile([P, S], U32, name)
+            for u in range(2):
+                nc.vector.tensor_copy(picked[u][:], table[:].bitcast(U32).indirect(offsets[:, 16 * u : 16 * (u + 1)]))
+            for u in range(2):
+                nc.vector.tensor_copy(
+                    words[:].rearrange("p (j u c i) -> p u c j i", j=PACK, u=2, i=4)[:, u],
+                    picked[u][:].rearrange("p (c i j) -> p c j i", j=PACK, i=4),
+                )
+            return words
 
         def woven(ap):
-            return ap.rearrange("p (c i j) -> p c j i", i=4, j=PACK)
+            return ap.rearrange("p (c i j) -> p c j i", i=2, j=PACK)
 
         def planar(ap):
-            return ap.rearrange("p j (c i) -> p c j i", i=4)
+            return ap.rearrange("p j (c i) -> p c j i", i=2)
 
         def cast(name, raw_cols, scale):
             width = raw_cols.shape[2]
@@ -126,10 +132,10 @@ def tile_picked_yaflow_step_p_kernel(
         sig_scales = [tile([P, 2 * 3 * QUART], U8, "sig_scales%d" % h) for h in range(2)]
 
         def sig_slot(h, slot):
-            return sig_bf[h][:].rearrange("p (q s c i j) -> p q s c j i", q=2, s=3, i=4, j=PACK)[:, :, slot]
+            return sig_bf[h][:].rearrange("p (q s c i j) -> p q s c j i", q=2, s=3, i=2, j=PACK)[:, :, slot]
 
         def sig_src(raw, h):
-            return raw[:, :, halves[h]].rearrange("p j (q c i) -> p q c j i", q=2, i=4)
+            return raw[:, :, halves[h]].rearrange("p j (q c i) -> p q c j i", q=2, i=2)
 
         def cast_xi(h):
             nc.scalar.copy(sig_slot(h, XI), sig_src(xi_raw, h))
@@ -147,8 +153,8 @@ def tile_picked_yaflow_step_p_kernel(
         deal_scales(slice(S, 2 * S), es_picked)
         for h in range(2):
             nc.scalar.copy(sig_slot(h, XR), sig_src(xr_raw, h))
-        for i in range(4):
-            nc.scalar.dma_start(planes[i:P:32, :].bitcast(I32), dealt[8 * i : P : 32, :].bitcast(I32))
+        for i in range(1, 4):
+            nc.scalar.dma_start(dealt[i:P:32, :].bitcast(I32), dealt[8 * i : P : 32, :].bitcast(I32))
         cur_sb = tile([P, R // P, N], F32, "cur_sb", "xr_raw")
         nc.sync.dma_start(cur_sb[:], cur.rearrange("(t p) m -> p t m", p=P))
         xw = gather_words("xw", xw_table)
@@ -160,8 +166,8 @@ def tile_picked_yaflow_step_p_kernel(
         amp_sb = load_rows("amp_sb", amp, "xi_raw")
         quantize_sig(1, 0, 256)
         quantize_sig(1, 256, 384)
-        x_q = (xw, planes[:, :S])
-        e_q = (ew, planes[:, S:])
+        x_q = (xw, dealt[:, :S])
+        e_q = (ew, dealt[:, S:])
 
         field = []
         for q in range(4):

@@ -27,9 +27,12 @@ def tile_picked_yaflow_step_p_kernel(
     nc = tc.nc
     with ExitStack() as ctx:
         sb = ctx.enter_context(tc.tile_pool(name="sb", bufs=1))
+        words_pool = ctx.enter_context(tc.tile_pool(name="words", bufs=1))
         ps = ctx.enter_context(tc.psum_pool(name="ps", bufs=1))
 
-        def tile(shape, dtype, name, tag=None):
+        def tile(shape, dtype, name, tag=None, offset=None):
+            if offset is not None:
+                return words_pool.tile(shape, dtype, name=name, align_bytes=64, offset=offset)
             return sb.tile(shape, dtype, name=name, tag=tag or name, align_bytes=64)
 
         def cleared(name, width, clear):
@@ -50,13 +53,13 @@ def tile_picked_yaflow_step_p_kernel(
         def load_scales(table, scales):
             nc.sync.dma_start(table[0:P:8, :].bitcast(I32), scales[0].bitcast(I32))
 
-        def load_words(name, words):
-            table = tile([P, T], I32, name)
+        def load_words(name, words, offset):
+            table = tile([P, T], I32, name, offset=offset)
             nc.sync.dma_start(table[:], words[0].rearrange("p c b -> p (c b)").bitcast(I32))
             return table
 
-        def load_rows(name, rows, tag=None):
-            raw = tile([P, PACK, rows.shape[1]], F32, name, tag)
+        def load_rows(name, rows, tag=None, offset=None):
+            raw = tile([P, PACK, rows.shape[1]], F32, name, tag, offset)
             nc.sync.dma_start(raw[:], rows.rearrange("(p j) c -> p j c", j=PACK))
             return raw
 
@@ -65,11 +68,10 @@ def tile_picked_yaflow_step_p_kernel(
         load_scales(xs_table, x_scales)
         load_scales(es_table, e_scales)
         xr_raw = load_rows("xr_raw", xr)
-        xw_table = load_words("xw_table", x_words)
+        xw_table = load_words("xw_table", x_words, 0)
         xi_raw = load_rows("xi_raw", xi)
-        ew_table = load_words("ew_table", e_words)
+        ew_table = load_words("ew_table", e_words, 4 * T)
         br_raw = load_rows("br_raw", br)
-        bi_raw = load_rows("bi_raw", bi)
         neg_w = tile([P, PACK, 1], F32, "neg_w")
         nc.gpsimd.tensor_scalar(neg_w[:], w_sb[:], -1.0, 0.0, ALU.mult, ALU.add)
         dealt = tile([P, 2 * S], U8, "dealt")
@@ -83,15 +85,8 @@ def tile_picked_yaflow_step_p_kernel(
             nc.vector.tensor_copy(dealt[:, cols].rearrange("p (j q) -> p j q", j=PACK), picked[:].rearrange("p (q j) -> p j q", j=PACK))
 
         def gather_words(name, table):
-            picked = [tile([P, S // 2], U32, name + "_picked%d" % u) for u in range(2)]
             words = tile([P, S], U32, name)
-            for u in range(2):
-                nc.vector.tensor_copy(picked[u][:], table[:].bitcast(U32).indirect(offsets[:, 16 * u : 16 * (u + 1)]))
-            for u in range(2):
-                nc.vector.tensor_copy(
-                    words[:].rearrange("p (j u c i) -> p u c j i", j=PACK, u=2, i=4)[:, u],
-                    picked[u][:].rearrange("p (c i j) -> p c j i", j=PACK, i=4),
-                )
+            nc.vector.tensor_copy(words[:].rearrange("p (j q) -> p q j", j=PACK), table[:].bitcast(U32).indirect(offsets[:]))
             return words
 
         def woven(ap):
@@ -128,7 +123,7 @@ def tile_picked_yaflow_step_p_kernel(
         quarters = [slice(q * QUART, (q + 1) * QUART) for q in range(N // QUART)]
         NEG_XI, XR, XI = 0, 1, 2
         sig_bf = [tile([P, 2 * 3 * QUART * PACK], BF16, "sig_bf%d" % h) for h in range(2)]
-        sig_codes = [tile([P, 2 * 3 * QUART], U32, "sig_codes%d" % h) for h in range(2)]
+        sig_codes = [tile([P, 2 * 3 * QUART], U32, "sig_codes0"), tile([P, 2 * 3 * QUART], U32, "sig_codes1", offset=4 * T)]
         sig_scales = [tile([P, 2 * 3 * QUART], U8, "sig_scales%d" % h) for h in range(2)]
 
         def sig_slot(h, slot):
@@ -154,16 +149,20 @@ def tile_picked_yaflow_step_p_kernel(
         for h in range(2):
             nc.scalar.copy(sig_slot(h, XR), sig_src(xr_raw, h))
         for i in range(1, 4):
-            nc.scalar.dma_start(dealt[i:P:32, :].bitcast(I32), dealt[8 * i : P : 32, :].bitcast(I32))
-        cur_sb = tile([P, R // P, N], F32, "cur_sb", "xr_raw")
-        nc.sync.dma_start(cur_sb[:], cur.rearrange("(t p) m -> p t m", p=P))
+            nc.sync.dma_start(dealt[i:P:32, :].bitcast(I32), dealt[8 * i : P : 32, :].bitcast(I32))
+        bi_raw = load_rows("bi_raw", bi, "es_picked")
         xw = gather_words("xw", xw_table)
+        amp_sb = load_rows("amp_sb", amp, offset=0)
+        warm_ps = ps.tile([P, S], F32, name="warm_ps", tag="acc1_1")
+        for width in (512, 512, 256):
+            mm(warm_ps[:, :width], (xw, xs_picked), slice(0, P), (xw, xs_picked), slice(0, width), True, True)
         cast_xi(0)
         quantize_sig(0, 0, 256)
         quantize_sig(0, 256, 384)
         ew = gather_words("ew", ew_table)
         cast_xi(1)
-        amp_sb = load_rows("amp_sb", amp, "xi_raw")
+        cur_sb = tile([P, R // P, N], F32, "cur_sb", offset=5 * T)
+        nc.sync.dma_start(cur_sb[:], cur.rearrange("(t p) m -> p t m", p=P))
         quantize_sig(1, 0, 256)
         quantize_sig(1, 256, 384)
         x_q = (xw, dealt[:, :S])
@@ -206,7 +205,7 @@ def tile_picked_yaflow_step_p_kernel(
             nc.vector.tensor_tensor(ratio[q][:], inv[q][:], amp_sb[:, :, quarters[q]], ALU.mult)
 
         def coefficient(q):
-            if q < 2:
+            if q < 1:
                 nc.vector.scalar_tensor_tensor(coef[q][:], ratio[q][:], 1.0, neg_w[:].to_broadcast([P, PACK, QUART]), ALU.subtract, ALU.mult)
                 return
             for j in range(PACK):
@@ -222,8 +221,16 @@ def tile_picked_yaflow_step_p_kernel(
                     ALU.mult,
                 )
 
+        z_codes = [tile([P, 2 * HALF], U32, "z_codes%d" % h) for h in range(2)]
+        z_scales = [tile([P, 2 * HALF], U8, "z_scales%d" % h) for h in range(2)]
+
+        def quantize_z(h, lo, hi):
+            nc.vector.quantize_mx(
+                out=z_codes[h][:, lo:hi].bitcast(FP8X4), scales=z_scales[h][:, lo:hi], in_=z_bf[h][:, lo * PACK : hi * PACK]
+            )
+
         def back(h):
-            z_h = quantize("z_q%d" % h, z_bf[h])
+            z_h = (z_codes[h], z_scales[h])
             accs = []
             for t in range(R // P):
                 rows = slice(t * P, (t + 1) * P)
@@ -244,28 +251,33 @@ def tile_picked_yaflow_step_p_kernel(
         add_squares(0)
         b_q.append(quantize("bi_q", bi_bf))
         square(1)
-        inverse_root(0)
         add_squares(1)
-        amp_ratio(0)
         square(2)
-        inverse_root(1)
+        inverse_root(0)
         add_squares(2)
+        amp_ratio(0)
+        square(3)
+        inverse_root(1)
+        add_squares(3)
         coefficient(0)
         amp_ratio(1)
-        square(3)
         inverse_root(2)
-        add_squares(3)
+        inverse_root(3)
         coefficient(1)
         amp_ratio(2)
-        inverse_root(3)
         residual(0)
-        coefficient(2)
         amp_ratio(3)
-        residual(1)
+        coefficient(2)
         coefficient(3)
+        residual(1)
         residual(2)
+        quantize_z(0, 0, 2 * HALF)
         back(0)
+        quantize_z(1, 0, QUART)
+        quantize_z(1, HALF, HALF + QUART)
         residual(3)
+        quantize_z(1, QUART, HALF)
+        quantize_z(1, HALF + QUART, 2 * HALF)
         finish(0)
         back(1)
         finish(1)

@@ -17,8 +17,15 @@ ALU = mybir.AluOpType
 
 P = 128
 PACK = 4
+BLOCK_PARTITIONS = 8
+QUADRANT = 32
 HALF = 128
-QUART = 64
+QUARTER = 64
+NEG_XI, XR, XI = 0, 1, 2
+PARTS = 3
+HALF_WORDS = 2 * PARTS * QUARTER
+TABLE_BYTES = 4 * T
+PAIR = 2
 
 
 def tile_picked_yaflow_step_p_kernel(
@@ -35,23 +42,13 @@ def tile_picked_yaflow_step_p_kernel(
                 return words_pool.tile(shape, dtype, name=name, align_bytes=64, offset=offset)
             return sb.tile(shape, dtype, name=name, tag=tag or name, align_bytes=64)
 
-        def cleared(name, width, clear):
-            table = tile([P, width], U8, name)
-            clear.memset(table[:].bitcast(I32), 0)
+        def cleared(name, engine):
+            table = tile([P, T], U8, name)
+            engine.memset(table[:].bitcast(I32), 0)
             return table
 
-        offsets = sb.tile([P, S // 16], U16, name="offsets")
-        nc.sync.dma_start(offsets[:], offs)
-
-        xs_table = cleared("xs_table", T, nc.vector)
-        es_table = cleared("es_table", T, nc.gpsimd)
-        one = tile([P, 1], F32, "one")
-        warm = tile([P, 1], F32, "warm")
-        nc.vector.memset(one[:], 1.0)
-        nc.scalar.activation(warm[:], one[:], ACT.Abs_reciprocal_sqrt)
-
         def load_scales(table, scales):
-            nc.sync.dma_start(table[0:P:8, :].bitcast(I32), scales[0].bitcast(I32))
+            nc.sync.dma_start(table[0:P:BLOCK_PARTITIONS, :].bitcast(I32), scales[0].bitcast(I32))
 
         def load_words(name, words, offset):
             table = tile([P, T], I32, name, offset=offset)
@@ -63,6 +60,16 @@ def tile_picked_yaflow_step_p_kernel(
             nc.sync.dma_start(raw[:], rows.rearrange("(p j) c -> p j c", j=PACK))
             return raw
 
+        offsets = sb.tile([P, S // 16], U16, name="offsets")
+        nc.sync.dma_start(offsets[:], offs)
+        xs_table = cleared("xs_table", nc.vector)
+        es_table = cleared("es_table", nc.gpsimd)
+
+        one = tile([P, 1], F32, "one")
+        warm = tile([P, 1], F32, "warm")
+        nc.vector.memset(one[:], 1.0)
+        nc.scalar.activation(warm[:], one[:], ACT.Abs_reciprocal_sqrt)
+
         w_sb = tile([P, PACK, 1], F32, "w_sb")
         nc.sync.dma_start(w_sb[:], wgt.rearrange("(p j) o -> p j o", j=PACK))
         load_scales(xs_table, x_scales)
@@ -70,7 +77,7 @@ def tile_picked_yaflow_step_p_kernel(
         xr_raw = load_rows("xr_raw", xr)
         xw_table = load_words("xw_table", x_words, 0)
         xi_raw = load_rows("xi_raw", xi)
-        ew_table = load_words("ew_table", e_words, 4 * T)
+        ew_table = load_words("ew_table", e_words, TABLE_BYTES)
         br_raw = load_rows("br_raw", br)
         neg_w = tile([P, PACK, 1], F32, "neg_w")
         nc.gpsimd.tensor_scalar(neg_w[:], w_sb[:], -1.0, 0.0, ALU.mult, ALU.add)
@@ -82,24 +89,22 @@ def tile_picked_yaflow_step_p_kernel(
             return picked
 
         def deal_scales(cols, picked):
-            nc.vector.tensor_copy(dealt[:, cols].rearrange("p (j q) -> p j q", j=PACK), picked[:].rearrange("p (q j) -> p j q", j=PACK))
+            nc.vector.tensor_copy(
+                dealt[:, cols].rearrange("p (j q) -> p j q", j=PACK), picked[:].rearrange("p (q j) -> p j q", j=PACK)
+            )
 
         def gather_words(name, table):
             words = tile([P, S], U32, name)
-            nc.vector.tensor_copy(words[:].rearrange("p (j q) -> p q j", j=PACK), table[:].bitcast(U32).indirect(offsets[:]))
+            nc.vector.tensor_copy(
+                words[:].rearrange("p (j q) -> p q j", j=PACK), table[:].bitcast(U32).indirect(offsets[:])
+            )
             return words
 
         def woven(ap):
-            return ap.rearrange("p (c i j) -> p c j i", i=2, j=PACK)
+            return ap.rearrange("p (c i j) -> p c j i", i=PAIR, j=PACK)
 
         def planar(ap):
-            return ap.rearrange("p j (c i) -> p c j i", i=2)
-
-        def cast(name, raw_cols, scale):
-            width = raw_cols.shape[2]
-            grouped = tile([P, width * PACK], BF16, name)
-            nc.scalar.activation(woven(grouped[:]), planar(raw_cols), ACT.Copy, scale=scale)
-            return grouped
+            return ap.rearrange("p j (c i) -> p c j i", i=PAIR)
 
         def quantize(name, grouped):
             width = grouped.shape[1] // PACK
@@ -120,26 +125,28 @@ def tile_picked_yaflow_step_p_kernel(
             )
 
         halves = [slice(h * HALF, (h + 1) * HALF) for h in range(N // HALF)]
-        quarters = [slice(q * QUART, (q + 1) * QUART) for q in range(N // QUART)]
-        NEG_XI, XR, XI = 0, 1, 2
-        sig_bf = [tile([P, 2 * 3 * QUART * PACK], BF16, "sig_bf%d" % h) for h in range(2)]
-        sig_codes = [tile([P, 2 * 3 * QUART], U32, "sig_codes0"), tile([P, 2 * 3 * QUART], U32, "sig_codes1", offset=4 * T)]
-        sig_scales = [tile([P, 2 * 3 * QUART], U8, "sig_scales%d" % h) for h in range(2)]
+        quarters = [slice(q * QUARTER, (q + 1) * QUARTER) for q in range(N // QUARTER)]
 
-        def sig_slot(h, slot):
-            return sig_bf[h][:].rearrange("p (q s c i j) -> p q s c j i", q=2, s=3, i=2, j=PACK)[:, :, slot]
+        sig_bf = [tile([P, HALF_WORDS * PACK], BF16, "sig_bf%d" % h) for h in range(2)]
+        sig_codes = [tile([P, HALF_WORDS], U32, "sig_codes0"), tile([P, HALF_WORDS], U32, "sig_codes1", offset=TABLE_BYTES)]
+        sig_scales = [tile([P, HALF_WORDS], U8, "sig_scales%d" % h) for h in range(2)]
+
+        def sig_part(h, part):
+            return sig_bf[h][:].rearrange("p (q s c i j) -> p q s c j i", q=2, s=PARTS, i=PAIR, j=PACK)[:, :, part]
 
         def sig_src(raw, h):
-            return raw[:, :, halves[h]].rearrange("p j (q c i) -> p q c j i", q=2, i=2)
+            return raw[:, :, halves[h]].rearrange("p j (q c i) -> p q c j i", q=2, i=PAIR)
 
         def cast_xi(h):
-            nc.scalar.copy(sig_slot(h, XI), sig_src(xi_raw, h))
+            nc.scalar.copy(sig_part(h, XI), sig_src(xi_raw, h))
             for q in range(2):
-                nc.scalar.activation(sig_slot(h, NEG_XI)[:, q], sig_src(xi_raw, h)[:, q], ACT.Copy, scale=-1.0)
+                nc.scalar.activation(sig_part(h, NEG_XI)[:, q], sig_src(xi_raw, h)[:, q], ACT.Copy, scale=-1.0)
 
         def quantize_sig(h, lo, hi):
             nc.vector.quantize_mx(
-                out=sig_codes[h][:, lo:hi].bitcast(FP8X4), scales=sig_scales[h][:, lo:hi], in_=sig_bf[h][:, lo * PACK : hi * PACK]
+                out=sig_codes[h][:, lo:hi].bitcast(FP8X4),
+                scales=sig_scales[h][:, lo:hi],
+                in_=sig_bf[h][:, lo * PACK : hi * PACK],
             )
 
         xs_picked = gather_scales("xs_picked", xs_table)
@@ -147,56 +154,62 @@ def tile_picked_yaflow_step_p_kernel(
         deal_scales(slice(0, S), xs_picked)
         deal_scales(slice(S, 2 * S), es_picked)
         for h in range(2):
-            nc.scalar.copy(sig_slot(h, XR), sig_src(xr_raw, h))
-        for i in range(1, 4):
-            nc.sync.dma_start(dealt[i:P:32, :].bitcast(I32), dealt[8 * i : P : 32, :].bitcast(I32))
+            nc.scalar.copy(sig_part(h, XR), sig_src(xr_raw, h))
+        for i in range(1, QUADRANT // BLOCK_PARTITIONS):
+            nc.sync.dma_start(
+                dealt[i:P:QUADRANT, :].bitcast(I32), dealt[BLOCK_PARTITIONS * i : P : QUADRANT, :].bitcast(I32)
+            )
         bi_raw = load_rows("bi_raw", bi, "es_picked")
         xw = gather_words("xw", xw_table)
         amp_sb = load_rows("amp_sb", amp, offset=0)
-        warm_ps = ps.tile([P, S], F32, name="warm_ps", tag="acc1_1")
-        for width in (512, 512, 256):
-            mm(warm_ps[:, :width], (xw, xs_picked), slice(0, P), (xw, xs_picked), slice(0, width), True, True)
         cast_xi(0)
-        quantize_sig(0, 0, 256)
-        quantize_sig(0, 256, 384)
+        quantize_sig(0, 0, 2 * QUARTER)
+        warm_ps = ps.tile([P, S], F32, name="warm_ps", tag="acc1_1")
+        for width in (S, S, S // 2):
+            mm(warm_ps[:, :width], (sig_codes[0], sig_scales[0]), slice(0, P), (xw, xs_picked), slice(0, width), True, True)
+        quantize_sig(0, 2 * QUARTER, HALF_WORDS)
         ew = gather_words("ew", ew_table)
         cast_xi(1)
-        cur_sb = tile([P, R // P, N], F32, "cur_sb", offset=5 * T)
+        cur_sb = tile([P, R // P, N], F32, "cur_sb", offset=TABLE_BYTES + TABLE_BYTES // 4)
         nc.sync.dma_start(cur_sb[:], cur.rearrange("(t p) m -> p t m", p=P))
-        quantize_sig(1, 0, 256)
-        quantize_sig(1, 256, 384)
+        quantize_sig(1, 0, 4 * QUARTER)
+        quantize_sig(1, 4 * QUARTER, HALF_WORDS)
         x_q = (xw, dealt[:, :S])
         e_q = (ew, dealt[:, S:])
 
         field = []
-        for q in range(4):
+        for q in range(len(quarters)):
             sig_q = (sig_codes[q // 2], sig_scales[q // 2])
-            base = (q % 2) * 3 * QUART
-            bank = ps.tile([P, PACK, 2 * QUART], F32, name="field%d" % q)
+            base = (q % 2) * PARTS * QUARTER
+            xr_xi = slice(base + XR * QUARTER, base + (XI + 1) * QUARTER)
+            neg_xi_xr = slice(base + NEG_XI * QUARTER, base + (XR + 1) * QUARTER)
+            bank = ps.tile([P, PACK, 2 * QUARTER], F32, name="field%d" % q)
             for j in range(PACK):
-                rows = slice(j * P, (j + 1) * P)
-                mm(bank[:, j, :], x_q, rows, sig_q, slice(base + QUART, base + 3 * QUART), True, False)
-                mm(bank[:, j, :], e_q, rows, sig_q, slice(base, base + 2 * QUART), False, True)
+                entries = slice(j * P, (j + 1) * P)
+                mm(bank[:, j, :], x_q, entries, sig_q, xr_xi, True, False)
+                mm(bank[:, j, :], e_q, entries, sig_q, neg_xi_xr, False, True)
             field.append(bank)
 
-        br_q = quantize("br_q", cast("br_bf", br_raw[:], 1.0))
+        br_bf = tile([P, R * PACK], BF16, "br_bf")
+        nc.scalar.activation(woven(br_bf[:]), planar(br_raw[:]), ACT.Copy, scale=1.0)
+        br_q = quantize("br_q", br_bf)
         bi_bf = tile([P, R * PACK], BF16, "bi_bf")
         nc.vector.tensor_copy(woven(bi_bf[:]), planar(bi_raw[:]))
 
-        squares = [tile([P, PACK, 2 * QUART], F32, "squares%d" % q) for q in range(4)]
-        power = [tile([P, PACK, QUART], F32, "power%d" % q) for q in range(4)]
-        inv = [tile([P, PACK, QUART], F32, "inv%d" % q) for q in range(4)]
-        ratio = [tile([P, PACK, QUART], F32, "ratio%d" % q) for q in range(4)]
-        coef = [tile([P, PACK, QUART], F32, "coef%d" % q) for q in range(4)]
+        squares = [tile([P, PACK, 2 * QUARTER], F32, "squares%d" % q) for q in range(4)]
+        power = [tile([P, PACK, QUARTER], F32, "power%d" % q) for q in range(4)]
+        inv = [tile([P, PACK, QUARTER], F32, "inv%d" % q) for q in range(4)]
+        ratio = [tile([P, PACK, QUARTER], F32, "ratio%d" % q) for q in range(4)]
+        coef = [tile([P, PACK, QUARTER], F32, "coef%d" % q) for q in range(4)]
         z_bf = [tile([P, 2 * HALF * PACK], BF16, "z_bf%d" % h) for h in range(2)]
-        b_q = [br_q]
-        z_q = []
 
         def square(q):
             nc.scalar.activation(squares[q][:], field[q][:], ACT.Square)
 
         def add_squares(q):
-            nc.vector.scalar_tensor_tensor(power[q][:], squares[q][:, :, :QUART], 0.1, squares[q][:, :, QUART:], ALU.add, ALU.add)
+            nc.vector.scalar_tensor_tensor(
+                power[q][:], squares[q][:, :, :QUARTER], 0.1, squares[q][:, :, QUARTER:], ALU.add, ALU.add
+            )
 
         def inverse_root(q):
             nc.scalar.activation(inv[q][:], power[q][:], ACT.Abs_reciprocal_sqrt)
@@ -204,19 +217,22 @@ def tile_picked_yaflow_step_p_kernel(
         def amp_ratio(q):
             nc.vector.tensor_tensor(ratio[q][:], inv[q][:], amp_sb[:, :, quarters[q]], ALU.mult)
 
-        def coefficient(q):
-            if q < 1:
-                nc.vector.scalar_tensor_tensor(coef[q][:], ratio[q][:], 1.0, neg_w[:].to_broadcast([P, PACK, QUART]), ALU.subtract, ALU.mult)
-                return
+        def coefficient_on_vector(q):
+            spread = neg_w[:].to_broadcast([P, PACK, QUARTER])
+            nc.vector.scalar_tensor_tensor(coef[q][:], ratio[q][:], 1.0, spread, ALU.subtract, ALU.mult)
+
+        def coefficient_on_scalar(q):
             for j in range(PACK):
-                nc.scalar.activation(coef[q][:, j, :], ratio[q][:, j, :], ACT.Identity, bias=w_sb[:, j, :], scale=neg_w[:, j, :])
+                nc.scalar.activation(
+                    coef[q][:, j, :], ratio[q][:, j, :], ACT.Identity, bias=w_sb[:, j, :], scale=neg_w[:, j, :]
+                )
 
         def residual(q):
             for s in range(2):
-                lo = (s * HALF + (q % 2) * QUART) * PACK
+                lo = (s * HALF + (q % 2) * QUARTER) * PACK
                 nc.vector.tensor_tensor(
-                    woven(z_bf[q // 2][:, lo : lo + QUART * PACK]),
-                    planar(field[q][:, :, s * QUART : (s + 1) * QUART]),
+                    woven(z_bf[q // 2][:, lo : lo + QUARTER * PACK]),
+                    planar(field[q][:, :, s * QUARTER : (s + 1) * QUARTER]),
                     planar(coef[q][:]),
                     ALU.mult,
                 )
@@ -226,30 +242,36 @@ def tile_picked_yaflow_step_p_kernel(
 
         def quantize_z(h, lo, hi):
             nc.vector.quantize_mx(
-                out=z_codes[h][:, lo:hi].bitcast(FP8X4), scales=z_scales[h][:, lo:hi], in_=z_bf[h][:, lo * PACK : hi * PACK]
+                out=z_codes[h][:, lo:hi].bitcast(FP8X4),
+                scales=z_scales[h][:, lo:hi],
+                in_=z_bf[h][:, lo * PACK : hi * PACK],
             )
 
-        def back(h):
+        def quantize_quarter(q):
+            for s in range(2):
+                lo = s * HALF + (q % 2) * QUARTER
+                quantize_z(q // 2, lo, lo + QUARTER)
+
+        def back_project(h, bi_q):
             z_h = (z_codes[h], z_scales[h])
-            accs = []
+            sums = []
             for t in range(R // P):
                 rows = slice(t * P, (t + 1) * P)
                 acc = ps.tile([P, HALF], F32, name="acc%d_%d" % (h, t))
-                mm(acc[:], b_q[0], rows, z_h, slice(0, HALF), True, False)
-                mm(acc[:], b_q[1], rows, z_h, slice(HALF, 2 * HALF), False, True)
-                accs.append(acc)
-            z_q.append(accs)
+                mm(acc[:], br_q, rows, z_h, slice(0, HALF), True, False)
+                mm(acc[:], bi_q, rows, z_h, slice(HALF, 2 * HALF), False, True)
+                sums.append(acc)
+            return sums
 
-        def finish(h):
-            for t in range(R // P):
+        def finish(h, sums):
+            for t, queue in enumerate((nc.sync, nc.scalar)):
                 res = tile([P, HALF], F32, "res%d_%d" % (h, t))
-                nc.vector.scalar_tensor_tensor(res[:], z_q[h][t][:], -0.5, cur_sb[:, t, halves[h]], ALU.mult, ALU.add)
-                queue = nc.sync if t == 0 else nc.scalar
+                nc.vector.scalar_tensor_tensor(res[:], sums[t][:], -0.5, cur_sb[:, t, halves[h]], ALU.mult, ALU.add)
                 queue.dma_start(out[t * P : (t + 1) * P, halves[h]], res[:])
 
         square(0)
         add_squares(0)
-        b_q.append(quantize("bi_q", bi_bf))
+        bi_q = quantize("bi_q", bi_bf)
         square(1)
         add_squares(1)
         square(2)
@@ -259,25 +281,22 @@ def tile_picked_yaflow_step_p_kernel(
         square(3)
         inverse_root(1)
         add_squares(3)
-        coefficient(0)
+        coefficient_on_vector(0)
         amp_ratio(1)
         inverse_root(2)
         inverse_root(3)
-        coefficient(1)
+        coefficient_on_scalar(1)
         amp_ratio(2)
         residual(0)
         amp_ratio(3)
-        coefficient(2)
-        coefficient(3)
+        coefficient_on_scalar(2)
+        coefficient_on_scalar(3)
         residual(1)
         residual(2)
         quantize_z(0, 0, 2 * HALF)
-        back(0)
-        quantize_z(1, 0, QUART)
-        quantize_z(1, HALF, HALF + QUART)
+        first_sums = back_project(0, bi_q)
+        quantize_quarter(2)
         residual(3)
-        quantize_z(1, QUART, HALF)
-        quantize_z(1, HALF + QUART, 2 * HALF)
-        finish(0)
-        back(1)
-        finish(1)
+        quantize_quarter(3)
+        finish(0, first_sums)
+        finish(1, back_project(1, bi_q))

from contextlib import ExitStack

import concourse.mybir as mybir

K, T, S, N, R = 512, 2048, 512, 256, 256
FLOPS = 2 * (4 * K * S * N + 2 * S * R * N)

F32 = mybir.dt.float32
BF16 = mybir.dt.bfloat16
I32 = mybir.dt.int32
U32 = mybir.dt.uint32
U16 = mybir.dt.uint16
U8 = mybir.dt.uint8
FP8X4 = mybir.dt.float8_e4m3fn_x4
ACT = mybir.ActivationFunctionType
ALU = mybir.AluOpType

P = 128
PACK = 4
BLOCK_PARTITIONS = 8
QUADRANT = 32
HALF = 128
QUARTER = 64
NEG_XI, XR, XI = 0, 1, 2
PARTS = 3
HALF_WORDS = 2 * PARTS * QUARTER
TABLE_BYTES = 4 * T
PAIR = 2


def tile_picked_yaflow_step_p_kernel(
    tc, x_words, x_scales, e_words, e_scales, xr, xi, amp, wgt, br, bi, cur, offs, out
):
    nc = tc.nc
    with ExitStack() as ctx:
        sb = ctx.enter_context(tc.tile_pool(name="sb", bufs=1))
        words_pool = ctx.enter_context(tc.tile_pool(name="words", bufs=1))
        ps = ctx.enter_context(tc.psum_pool(name="ps", bufs=1))

        def tile(shape, dtype, name, tag=None, offset=None):
            if offset is not None:
                return words_pool.tile(shape, dtype, name=name, align_bytes=64, offset=offset)
            return sb.tile(shape, dtype, name=name, tag=tag or name, align_bytes=64)

        def cleared(name, engine):
            table = tile([P, T], U8, name)
            engine.memset(table[:].bitcast(I32), 0)
            return table

        def load_scales(table, scales):
            nc.sync.dma_start(table[0:P:BLOCK_PARTITIONS, :].bitcast(I32), scales[0].bitcast(I32))

        def load_words(name, words, offset):
            table = tile([P, T], I32, name, offset=offset)
            nc.sync.dma_start(table[:], words[0].rearrange("p c b -> p (c b)").bitcast(I32))
            return table

        def load_rows(name, rows, tag=None, offset=None):
            raw = tile([P, PACK, rows.shape[1]], F32, name, tag, offset)
            nc.sync.dma_start(raw[:], rows.rearrange("(p j) c -> p j c", j=PACK))
            return raw

        offsets = sb.tile([P, S // 16], U16, name="offsets")
        nc.sync.dma_start(offsets[:], offs)
        xs_table = cleared("xs_table", nc.vector)
        es_table = cleared("es_table", nc.gpsimd)

        one = tile([P, 1], F32, "one")
        warm = tile([P, 1], F32, "warm")
        nc.vector.memset(one[:], 1.0)
        nc.scalar.activation(warm[:], one[:], ACT.Abs_reciprocal_sqrt)

        w_sb = tile([P, PACK, 1], F32, "w_sb")
        nc.sync.dma_start(w_sb[:], wgt.rearrange("(p j) o -> p j o", j=PACK))
        load_scales(xs_table, x_scales)
        load_scales(es_table, e_scales)
        xr_raw = load_rows("xr_raw", xr)
        xw_table = load_words("xw_table", x_words, 0)
        xi_raw = load_rows("xi_raw", xi)
        ew_table = load_words("ew_table", e_words, TABLE_BYTES)
        br_raw = load_rows("br_raw", br)
        neg_w = tile([P, PACK, 1], F32, "neg_w")
        nc.gpsimd.tensor_scalar(neg_w[:], w_sb[:], -1.0, 0.0, ALU.mult, ALU.add)
        dealt = tile([P, 2 * S], U8, "dealt")

        def gather_scales(name, table):
            picked = tile([P, S], U8, name)
            nc.vector.tensor_copy(picked[:], table[:].indirect(offsets[:]))
            return picked

        def deal_scales(cols, picked):
            nc.vector.tensor_copy(
                dealt[:, cols].rearrange("p (j q) -> p j q", j=PACK), picked[:].rearrange("p (q j) -> p j q", j=PACK)
            )

        def gather_words(name, table):
            words = tile([P, S], U32, name)
            nc.vector.tensor_copy(
                words[:].rearrange("p (j q) -> p q j", j=PACK), table[:].bitcast(U32).indirect(offsets[:])
            )
            return words

        def woven(ap):
            return ap.rearrange("p (c i j) -> p c j i", i=PAIR, j=PACK)

        def planar(ap):
            return ap.rearrange("p j (c i) -> p c j i", i=PAIR)

        def quantize(name, grouped):
            width = grouped.shape[1] // PACK
            codes = tile([P, width], U32, name + "_codes")
            scales = tile([P, width], U8, name + "_scales")
            nc.vector.quantize_mx(out=codes[:].bitcast(FP8X4), scales=scales[:], in_=grouped[:])
            return codes, scales

        def mm(acc, lhs, lhs_cols, rhs, rhs_cols, start, stop):
            nc.tensor.matmul_mx(
                out=acc,
                lhsT=lhs[0][:, lhs_cols].bitcast(FP8X4),
                lhsT_scale=lhs[1][:, lhs_cols],
                rhs=rhs[0][:, rhs_cols].bitcast(FP8X4),
                rhs_scale=rhs[1][:, rhs_cols],
                start=start,
                stop=stop,
            )

        halves = [slice(h * HALF, (h + 1) * HALF) for h in range(N // HALF)]
        quarters = [slice(q * QUARTER, (q + 1) * QUARTER) for q in range(N // QUARTER)]

        sig_bf = [tile([P, HALF_WORDS * PACK], BF16, "sig_bf%d" % h) for h in range(2)]
        sig_codes = [tile([P, HALF_WORDS], U32, "sig_codes0"), tile([P, HALF_WORDS], U32, "sig_codes1", offset=TABLE_BYTES)]
        sig_scales = [tile([P, HALF_WORDS], U8, "sig_scales%d" % h) for h in range(2)]

        def sig_part(h, part):
            return sig_bf[h][:].rearrange("p (q s c i j) -> p q s c j i", q=2, s=PARTS, i=PAIR, j=PACK)[:, :, part]

        def sig_src(raw, h):
            return raw[:, :, halves[h]].rearrange("p j (q c i) -> p q c j i", q=2, i=PAIR)

        def cast_xi(h):
            nc.scalar.copy(sig_part(h, XI), sig_src(xi_raw, h))
            for q in range(2):
                nc.scalar.activation(sig_part(h, NEG_XI)[:, q], sig_src(xi_raw, h)[:, q], ACT.Copy, scale=-1.0)

        def quantize_sig(h, lo, hi):
            nc.vector.quantize_mx(
                out=sig_codes[h][:, lo:hi].bitcast(FP8X4),
                scales=sig_scales[h][:, lo:hi],
                in_=sig_bf[h][:, lo * PACK : hi * PACK],
            )

        xs_picked = gather_scales("xs_picked", xs_table)
        es_picked = gather_scales("es_picked", es_table)
        deal_scales(slice(0, S), xs_picked)
        deal_scales(slice(S, 2 * S), es_picked)
        for h in range(2):
            nc.scalar.copy(sig_part(h, XR), sig_src(xr_raw, h))
        for i in range(1, QUADRANT // BLOCK_PARTITIONS):
            nc.sync.dma_start(
                dealt[i:P:QUADRANT, :].bitcast(I32), dealt[BLOCK_PARTITIONS * i : P : QUADRANT, :].bitcast(I32)
            )
        bi_raw = load_rows("bi_raw", bi, "es_picked")
        xw = gather_words("xw", xw_table)
        amp_sb = load_rows("amp_sb", amp, offset=0)
        cast_xi(0)
        quantize_sig(0, 0, 2 * QUARTER)
        warm_ps = ps.tile([P, S], F32, name="warm_ps", tag="acc1_1")
        for width in (S, S, S // 2):
            mm(warm_ps[:, :width], (sig_codes[0], sig_scales[0]), slice(0, P), (xw, xs_picked), slice(0, width), True, True)
        quantize_sig(0, 2 * QUARTER, HALF_WORDS)
        ew = gather_words("ew", ew_table)
        cast_xi(1)
        cur_sb = tile([P, R // P, N], F32, "cur_sb", offset=TABLE_BYTES + TABLE_BYTES // 4)
        nc.sync.dma_start(cur_sb[:], cur.rearrange("(t p) m -> p t m", p=P))
        quantize_sig(1, 0, 4 * QUARTER)
        quantize_sig(1, 4 * QUARTER, HALF_WORDS)
        x_q = (xw, dealt[:, :S])
        e_q = (ew, dealt[:, S:])

        field = []
        for q in range(len(quarters)):
            sig_q = (sig_codes[q // 2], sig_scales[q // 2])
            base = (q % 2) * PARTS * QUARTER
            xr_xi = slice(base + XR * QUARTER, base + (XI + 1) * QUARTER)
            neg_xi_xr = slice(base + NEG_XI * QUARTER, base + (XR + 1) * QUARTER)
            bank = ps.tile([P, PACK, 2 * QUARTER], F32, name="field%d" % q)
            for j in range(PACK):
                entries = slice(j * P, (j + 1) * P)
                mm(bank[:, j, :], x_q, entries, sig_q, xr_xi, True, False)
                mm(bank[:, j, :], e_q, entries, sig_q, neg_xi_xr, False, True)
            field.append(bank)

        br_bf = tile([P, R * PACK], BF16, "br_bf")
        nc.scalar.activation(woven(br_bf[:]), planar(br_raw[:]), ACT.Copy, scale=1.0)
        br_q = quantize("br_q", br_bf)
        bi_bf = tile([P, R * PACK], BF16, "bi_bf")
        nc.vector.tensor_copy(woven(bi_bf[:]), planar(bi_raw[:]))

        squares = [tile([P, PACK, 2 * QUARTER], F32, "squares%d" % q) for q in range(4)]
        power = [tile([P, PACK, QUARTER], F32, "power%d" % q) for q in range(4)]
        inv = [tile([P, PACK, QUARTER], F32, "inv%d" % q) for q in range(4)]
        ratio = [tile([P, PACK, QUARTER], F32, "ratio%d" % q) for q in range(4)]
        coef = [tile([P, PACK, QUARTER], F32, "coef%d" % q) for q in range(4)]
        z_bf = [tile([P, 2 * HALF * PACK], BF16, "z_bf%d" % h) for h in range(2)]

        def square(q):
            nc.scalar.activation(squares[q][:], field[q][:], ACT.Square)

        def add_squares(q):
            nc.vector.scalar_tensor_tensor(
                power[q][:], squares[q][:, :, :QUARTER], 0.1, squares[q][:, :, QUARTER:], ALU.add, ALU.add
            )

        def inverse_root(q):
            nc.scalar.activation(inv[q][:], power[q][:], ACT.Abs_reciprocal_sqrt)

        def amp_ratio(q):
            nc.vector.tensor_tensor(ratio[q][:], inv[q][:], amp_sb[:, :, quarters[q]], ALU.mult)

        def coefficient_on_vector(q):
            spread = neg_w[:].to_broadcast([P, PACK, QUARTER])
            nc.vector.scalar_tensor_tensor(coef[q][:], ratio[q][:], 1.0, spread, ALU.subtract, ALU.mult)

        def coefficient_on_scalar(q):
            for j in range(PACK):
                nc.scalar.activation(
                    coef[q][:, j, :], ratio[q][:, j, :], ACT.Identity, bias=w_sb[:, j, :], scale=neg_w[:, j, :]
                )

        def residual(q):
            for s in range(2):
                lo = (s * HALF + (q % 2) * QUARTER) * PACK
                nc.vector.tensor_tensor(
                    woven(z_bf[q // 2][:, lo : lo + QUARTER * PACK]),
                    planar(field[q][:, :, s * QUARTER : (s + 1) * QUARTER]),
                    planar(coef[q][:]),
                    ALU.mult,
                )

        z_codes = [tile([P, 2 * HALF], U32, "z_codes%d" % h) for h in range(2)]
        z_scales = [tile([P, 2 * HALF], U8, "z_scales%d" % h) for h in range(2)]

        def quantize_z(h, lo, hi):
            nc.vector.quantize_mx(
                out=z_codes[h][:, lo:hi].bitcast(FP8X4),
                scales=z_scales[h][:, lo:hi],
                in_=z_bf[h][:, lo * PACK : hi * PACK],
            )

        def quantize_quarter(q):
            for s in range(2):
                lo = s * HALF + (q % 2) * QUARTER
                quantize_z(q // 2, lo, lo + QUARTER)

        def back_project(h, bi_q):
            z_h = (z_codes[h], z_scales[h])
            sums = []
            for t in range(R // P):
                rows = slice(t * P, (t + 1) * P)
                acc = ps.tile([P, HALF], F32, name="acc%d_%d" % (h, t))
                mm(acc[:], br_q, rows, z_h, slice(0, HALF), True, False)
                mm(acc[:], bi_q, rows, z_h, slice(HALF, 2 * HALF), False, True)
                sums.append(acc)
            return sums

        def finish(h, sums):
            for t, queue in enumerate((nc.sync, nc.scalar)):
                res = tile([P, HALF], F32, "res%d_%d" % (h, t))
                nc.vector.scalar_tensor_tensor(res[:], sums[t][:], -0.5, cur_sb[:, t, halves[h]], ALU.mult, ALU.add)
                queue.dma_start(out[t * P : (t + 1) * P, halves[h]], res[:])

        square(0)
        add_squares(0)
        bi_q = quantize("bi_q", bi_bf)
        square(1)
        add_squares(1)
        square(2)
        inverse_root(0)
        add_squares(2)
        amp_ratio(0)
        square(3)
        inverse_root(1)
        add_squares(3)
        coefficient_on_vector(0)
        amp_ratio(1)
        inverse_root(2)
        inverse_root(3)
        coefficient_on_scalar(1)
        amp_ratio(2)
        residual(0)
        amp_ratio(3)
        coefficient_on_scalar(2)
        coefficient_on_scalar(3)
        residual(1)
        residual(2)
        quantize_z(0, 0, 2 * HALF)
        first_sums = back_project(0, bi_q)
        quantize_quarter(2)
        residual(3)
        quantize_quarter(3)
        finish(0, first_sums)
        finish(1, back_project(1, bi_q))
